import numpy as np
import ml_dtypes


def mxq(x, axis, fmt="e4m3"):
    dtype, down = {"e4m3": (ml_dtypes.float8_e4m3fn, 7), "e5m2": (ml_dtypes.float8_e5m2, 14)}[fmt]
    v = np.moveaxis(np.asarray(x, np.float32).astype(ml_dtypes.bfloat16).astype(np.float64), axis, -1)
    blocks = v.reshape(v.shape[:-1] + (-1, 32))
    amax = np.abs(blocks).max(-1, keepdims=True)
    byte = np.maximum(np.where(amax > 0, np.frexp(amax)[1] - 1 + 127, 0) - down, 1)
    scale = np.exp2(byte - 127.0)
    codes = (blocks / scale).astype(np.float32).astype(dtype).astype(np.float64)
    return np.moveaxis((codes * scale).reshape(v.shape), -1, axis)


WIDE = False


def mx_kscale(k):
    if not WIDE:
        return np.ones(k)
    levels = np.array([10, -10, 5, -5, 0])
    if k % 512:
        return np.exp2(np.random.permutation(np.resize(levels, k // 32))).repeat(32)
    a = np.empty((k // 512, 16))
    for p in range(k // 512):
        a[p, :8] = np.random.permutation(np.resize(levels, 8))
        for g in range(8):
            far = levels[np.abs(levels - a[p, g]) >= 10]
            a[p, g + 8] = far[np.random.randint(len(far))]
    return np.exp2(a.ravel()).repeat(32)


def f64(x):
    return np.asarray(x).astype(np.float64)


def striped(idx):
    return np.tile(idx.reshape(-1, 16).T, (8, 1)).astype(np.uint16)


def unstriped(offs):
    return offs[:16].T.reshape(-1).astype(np.int64)


def pack_weight(w):
    k, n = w.shape
    w = f64(np.asarray(w, np.float32).astype(ml_dtypes.bfloat16)).reshape(k // 32, 32, n)
    amax = np.abs(w).max(1)
    byte = np.clip(np.where(amax > 0, np.frexp(amax)[1] - 1 + 127 - 7, 1), 1, 254)
    scaled = (w * np.exp2(127.0 - byte)[:, None, :]).reshape(k, n).astype(np.float32)
    words = np.ascontiguousarray(scaled.reshape(k // 512, 128, 4, n).transpose(0, 1, 3, 2)).astype(ml_dtypes.float8_e4m3fn).view(np.uint8)
    return words, np.ascontiguousarray(byte.astype(np.uint8).reshape(k // 512, 16, n))


def unpack_weight(words, scales):
    g, p, n, _ = words.shape
    vals = np.ascontiguousarray(words).view(ml_dtypes.float8_e4m3fn).astype(np.float64) * np.repeat(np.exp2(scales.astype(np.float64) - 127.0), 8, axis=1)[..., None]
    return vals.transpose(0, 1, 3, 2).reshape(g * 512, n)


def silu(v):
    return v / (1.0 + np.exp(-np.maximum(v, -700.0)))


K, T, S, V, H, N = 1024, 1024, 512, 256, 512, 128


def setup_inputs():
    n = np.random.standard_normal
    s = mx_kscale(K)[:, None]
    u = mx_kscale(H)
    packed_xT = pack_weight(n((K, T)) * s)
    packed_w2 = pack_weight(n((H, N)) / np.sqrt(3 * H) / u[:, None])
    packed_w3 = pack_weight(n((H, N)) / np.sqrt(3 * H) / u[:, None])
    packed_w4 = pack_weight(n((H, N)) / np.sqrt(3 * H) / u[:, None])
    return {
        "x_words": packed_xT[0],
        "x_scales": packed_xT[1],
        "w1": (n((K, H)) / np.sqrt(K) / s * u).astype(np.float32),
        "w2_words": packed_w2[0],
        "w2_scales": packed_w2[1],
        "w3_words": packed_w3[0],
        "w3_scales": packed_w3[1],
        "w4_words": packed_w4[0],
        "w4_scales": packed_w4[1],
        "offs": striped(np.random.permutation(T)[:S]),
        "pos1": striped(np.random.permutation(S)[:V]),
        "pos2": striped(np.random.permutation(S)[:V]),
        "pos3": striped(np.random.permutation(S)[:V]),
    }


def reference(x_words, x_scales, w1, w2_words, w2_scales, w3_words, w3_scales, w4_words, w4_scales, offs, pos1, pos2, pos3):
    xq = unpack_weight(x_words, x_scales)[:, unstriped(offs)]
    h = silu(mxq(f64(w1), 0, "e4m3").T @ xq)
    g0 = h[:, unstriped(pos1)]
    g1 = h[:, unstriped(pos2)]
    g2 = h[:, unstriped(pos3)]
    z1 = (g0 + g1 + g2) / 3
    z2 = np.maximum(np.maximum(g0, g1), g2)
    z3 = np.minimum(np.minimum(g0, g1), g2)
    return unpack_weight(w2_words, w2_scales).T @ mxq(z1, 0, "e4m3") + unpack_weight(w3_words, w3_scales).T @ mxq(z2, 0, "e4m3") + unpack_weight(w4_words, w4_scales).T @ mxq(z3, 0, "e4m3")

@@ -1,0 +1,192 @@
+from contextlib import ExitStack
+
+import concourse.mybir as mybir
+from concourse.masks import make_identity
+
+K, T, S, V, H, N = 1024, 1024, 512, 256, 512, 128
+FLOPS = 2 * K * H * S + 3 * 2 * H * N * V
+
+F32 = mybir.dt.float32
+BF16 = mybir.dt.bfloat16
+I32 = mybir.dt.int32
+U32 = mybir.dt.uint32
+U16 = mybir.dt.uint16
+U8 = mybir.dt.uint8
+FP8X4 = mybir.dt.float8_e4m3fn_x4
+ACT = mybir.ActivationFunctionType
+ALU = mybir.AluOpType
+
+P = 128
+PACK = 4
+PASSES = K // (P * PACK)
+D = 3
+
+
+def tile_picked_pna_silu_p_kernel(
+    tc, x_words, x_scales, w1, w2_words, w2_scales, w3_words, w3_scales, w4_words, w4_scales,
+    offs, pos1, pos2, pos3, out,
+):
+    nc = tc.nc
+    with ExitStack() as ctx:
+        sb = ctx.enter_context(tc.tile_pool(name="sb", bufs=1))
+        ps = ctx.enter_context(tc.psum_pool(name="ps", bufs=1))
+
+        def tile(name, shape, dtype):
+            return sb.tile(shape, dtype, name=name, align_bytes=64)
+
+        offs_sb = tile("offs_sb", [P, S // 16], U16)
+        nc.sync.dma_start(offs_sb[:], offs)
+
+        xs_all = tile("xs_all", [P, T], U8)
+        nc.vector.memset(xs_all[:].bitcast(I32), 0)
+        ws_all = tile("ws_all", [P, D * N], U8)
+        nc.vector.memset(ws_all[:].bitcast(I32), 0)
+
+        xw_all = [tile("xw_all%d" % z, [P, T], U32) for z in range(PASSES)]
+        nc.sync.dma_start(xw_all[0][:].bitcast(I32), x_words[0].rearrange("p n t -> p (n t)").bitcast(I32))
+        for q in range(4):
+            nc.scalar.dma_start(
+                xs_all[32 * q : 32 * q + 4 * PASSES, :].bitcast(I32),
+                x_scales[:, 4 * q : 4 * q + 4, :].bitcast(I32),
+            )
+        nc.sync.dma_start(xw_all[1][:].bitcast(I32), x_words[1].rearrange("p n t -> p (n t)").bitcast(I32))
+
+        pieces = [(0, 0, H), (1, 0, H // 2), (1, H // 2, H)]
+        w1_raw = []
+        for z, c0, c1 in pieces:
+            raw = tile("w1_raw%d_%d" % (z, c0), [P, PACK, c1 - c0], F32)
+            nc.sync.dma_start(raw[:], w1[512 * z : 512 * (z + 1), c0:c1].rearrange("(p j) c -> p j c", j=PACK))
+            w1_raw.append(raw)
+
+        pos_sb = []
+        for d, pos in enumerate((pos1, pos2, pos3)):
+            lst = tile("pos_sb%d" % d, [P, V // 16], U16)
+            nc.sync.dma_start(lst[:], pos)
+            pos_sb.append(lst)
+
+        ww = []
+        for a, (words, scales) in enumerate(((w2_words, w2_scales), (w3_words, w3_scales), (w4_words, w4_scales))):
+            wt = tile("ww%d" % a, [P, N], U32)
+            nc.sync.dma_start(wt[:].bitcast(I32), words[0].rearrange("p n t -> p (n t)").bitcast(I32))
+            ww.append(wt)
+            for q in range(4):
+                nc.sync.dma_start(
+                    ws_all[32 * q : 32 * q + 4, a * N : (a + 1) * N].bitcast(I32),
+                    scales[0, 4 * q : 4 * q + 4, :].bitcast(I32),
+                )
+
+        ident = tile("ident", [P, P], F32)
+        make_identity(nc, ident[:])
+
+        xw = [tile("xw%d" % z, [P, S], U32) for z in range(PASSES)]
+        xs = tile("xs", [P, S], U8)
+        nc.vector.tensor_copy(xw[0][:], xw_all[0][:].indirect(offs_sb[:]))
+        nc.vector.tensor_copy(xs[:], xs_all[:].indirect(offs_sb[:]))
+        nc.vector.tensor_copy(xw[1][:], xw_all[1][:].indirect(offs_sb[:]))
+
+        wb = {}
+        wc = {}
+        wsc = {}
+        for z in range(PASSES):
+            for u in range(2):
+                wb[z, u] = tile("wb%d_%d" % (z, u), [P, 2, P, PACK], BF16)
+                wc[z, u] = tile("wc%d_%d" % (z, u), [P, 2 * P], U32)
+                wsc[z, u] = tile("wsc%d_%d" % (z, u), [P, 2 * P], U8)
+
+        def quantise_w1(z, u, e0, e1):
+            nc.vector.quantize_mx(
+                out=wc[z, u][:, e0 * P : e1 * P].bitcast(FP8X4),
+                scales=wsc[z, u][:, e0 * P : e1 * P],
+                in_=wb[z, u][:, e0:e1, :, :].rearrange("p e m j -> p (e m j)"),
+            )
+
+        acc = [ps.tile([P, S], F32, name="acc%d" % t) for t in range(PACK)]
+
+        def first_product(z, t):
+            u, e = divmod(t, 2)
+            nc.tensor.matmul_mx(
+                out=acc[t][:],
+                lhsT=wc[z, u][:, e * P : (e + 1) * P].bitcast(FP8X4),
+                lhsT_scale=wsc[z, u][:, e * P : (e + 1) * P],
+                rhs=xw[z][:].bitcast(FP8X4),
+                rhs_scale=xs[4 * z :, :],
+                start=(z == 0),
+                stop=(z == PASSES - 1),
+            )
+
+        for (z, c0, c1), raw in zip(pieces, w1_raw):
+            src = raw[:].rearrange("p j (m t) -> p m j t", t=PACK)
+            for u, copy in ((0, nc.vector.tensor_copy), (1, nc.scalar.copy)):
+                copy(
+                    wb[z, u][:, :, c0 // PACK : c1 // PACK, :].rearrange("p e m j -> p m j e"),
+                    src[:, :, :, 2 * u : 2 * u + 2],
+                )
+            if z == 0:
+                for u in range(2):
+                    quantise_w1(0, u, 0, 2)
+                for t in range(PACK):
+                    first_product(0, t)
+        quantise_w1(1, 0, 0, 1)
+        quantise_w1(1, 0, 1, 2)
+        quantise_w1(1, 1, 0, 2)
+
+        h = []
+        for t in range(PACK):
+            first_product(1, t)
+            ht = tile("h%d" % t, [P, S], F32)
+            nc.scalar.activation(ht[:], acc[t][:], ACT.Silu)
+            h.append(ht)
+
+        big01 = tile("big01", [P, 2, 2 * V], BF16)
+        small01 = tile("small01", [P, 2, 2 * V], BF16)
+        last = tile("last", [P, 2, 2 * V], BF16)
+        back = ps.tile([P, 2, V], F32, name="back")
+        for u in range(2):
+            g = [tile("g%d_%d" % (u, d), [P, 2, V], F32) for d in range(D)]
+            total = ps.tile([P, 2, 2, P], F32, name="total%d" % u)
+            for e in range(2):
+                for d in range(D):
+                    nc.vector.tensor_copy(g[d][:, e, :], h[2 * u + e][:].indirect(pos_sb[d][:]))
+                for half in range(2):
+                    for d in range(D):
+                        nc.tensor.matmul(
+                            total[:, half, e, :], lhsT=g[d][:, e, half * P : (half + 1) * P], rhs=ident[:],
+                            is_transpose=True, start=(d == 0), stop=(d == D - 1),
+                        )
+            gb = [tile("gb%d_%d" % (u, d), [P, 2 * V], BF16) for d in range(D - 1)]
+            for d, dst in enumerate((gb[0][:], gb[1][:], last[:, u, :])):
+                nc.scalar.copy(dst.rearrange("p (v e) -> p v e", e=2), g[d][:].rearrange("p e v -> p v e"))
+            nc.vector.tensor_tensor(big01[:, u, :], gb[0][:], gb[1][:], ALU.max)
+            nc.vector.tensor_tensor(small01[:, u, :], gb[0][:], gb[1][:], ALU.min)
+            mean_t = tile("mean_t%d" % u, [P, 2, P, 2], BF16)
+            nc.scalar.activation(mean_t[:], total[:].rearrange("v h e p -> v h p e"), ACT.Copy, scale=1.0 / D)
+            for half in range(2):
+                nc.tensor.transpose(
+                    back[:, u, half * P : (half + 1) * P],
+                    mean_t[:, half, :, :].rearrange("v p e -> v (p e)").bitcast(F32),
+                    ident[:],
+                )
+
+        zb = [tile("zb%d" % a, [P, PACK * V], BF16) for a in range(D)]
+        for a, part, op in ((1, big01, ALU.max), (2, small01, ALU.min)):
+            nc.vector.tensor_tensor(
+                zb[a][:].rearrange("p (v u e) -> p v u e", u=2, e=2),
+                part[:].rearrange("p u (v e) -> p v u e", e=2),
+                last[:].rearrange("p u (v e) -> p v u e", e=2),
+                op,
+            )
+        nc.scalar.copy(zb[0][:].bitcast(F32).rearrange("p (v u) -> p v u", u=2), back[:].rearrange("p u v -> p v u"))
+
+        res = ps.tile([P, V], F32, name="res")
+        order = (1, 2, 0)
+        for i, a in enumerate(order):
+            zc = tile("zc%d" % a, [P, V], U32)
+            zs = tile("zs%d" % a, [P, V], U8)
+            nc.vector.quantize_mx(out=zc[:].bitcast(FP8X4), scales=zs[:], in_=zb[a][:])
+            nc.tensor.matmul_mx(
+                out=res[:], lhsT=ww[a][:].bitcast(FP8X4), lhsT_scale=ws_all[:, a * N : (a + 1) * N],
+                rhs=zc[:].bitcast(FP8X4), rhs_scale=zs[:], start=(i == 0), stop=(i == D - 1),
+            )
+        res_sb = tile("res_sb", [P, V], F32)
+        nc.scalar.copy(res_sb[:], res[:])
+        nc.sync.dma_start(out, res_sb[:])

@@ -34,6 +34,11 @@ def tile_picked_pna_silu_p_kernel(
         def tile(name, shape, dtype):
             return sb.tile(shape, dtype, name=name, align_bytes=64)
 
+        warm_in = tile("warm_in", [P, 8], F32)
+        warm = tile("warm", [P, 8], F32)
+        nc.gpsimd.memset(warm_in[:], 0.0)
+        nc.scalar.activation(warm[:], warm_in[:], ACT.Silu)
+
         offs_sb = tile("offs_sb", [P, S // 16], U16)
         nc.sync.dma_start(offs_sb[:], offs)
 
@@ -45,18 +50,18 @@ def tile_picked_pna_silu_p_kernel(
         xw_all = [tile("xw_all%d" % z, [P, T], U32) for z in range(PASSES)]
         nc.sync.dma_start(xw_all[0][:].bitcast(I32), x_words[0].rearrange("p n t -> p (n t)").bitcast(I32))
         for q in range(4):
-            nc.scalar.dma_start(
+            nc.sync.dma_start(
                 xs_all[32 * q : 32 * q + 4 * PASSES, :].bitcast(I32),
                 x_scales[:, 4 * q : 4 * q + 4, :].bitcast(I32),
             )
-        nc.sync.dma_start(xw_all[1][:].bitcast(I32), x_words[1].rearrange("p n t -> p (n t)").bitcast(I32))
-
         pieces = [(0, 0, H), (1, 0, H // 2), (1, H // 2, H)]
         w1_raw = []
         for z, c0, c1 in pieces:
             raw = tile("w1_raw%d_%d" % (z, c0), [P, PACK, c1 - c0], F32)
             nc.sync.dma_start(raw[:], w1[512 * z : 512 * (z + 1), c0:c1].rearrange("(p j) c -> p j c", j=PACK))
             w1_raw.append(raw)
+            if z == 0:
+                nc.sync.dma_start(xw_all[1][:].bitcast(I32), x_words[1].rearrange("p n t -> p (n t)").bitcast(I32))
 
         pos_sb = []
         for d, pos in enumerate((pos1, pos2, pos3)):
@@ -82,7 +87,6 @@ def tile_picked_pna_silu_p_kernel(
         xs = tile("xs", [P, S], U8)
         nc.vector.tensor_copy(xw[0][:], xw_all[0][:].indirect(offs_sb[:]))
         nc.vector.tensor_copy(xs[:], xs_all[:].indirect(offs_sb[:]))
-        nc.vector.tensor_copy(xw[1][:], xw_all[1][:].indirect(offs_sb[:]))
 
         wb = {}
         wc = {}
@@ -122,16 +126,16 @@ def tile_picked_pna_silu_p_kernel(
                     src[:, :, :, 2 * u : 2 * u + 2],
                 )
             if z == 0:
-                for u in range(2):
-                    quantise_w1(0, u, 0, 2)
-                for t in range(PACK):
-                    first_product(0, t)
+                quantise_w1(0, 0, 0, 2)
+                nc.vector.tensor_copy(xw[1][:], xw_all[1][:].indirect(offs_sb[:]))
+                quantise_w1(0, 1, 0, 2)
         quantise_w1(1, 0, 0, 1)
         quantise_w1(1, 0, 1, 2)
         quantise_w1(1, 1, 0, 2)
 
         h = []
         for t in range(PACK):
+            first_product(0, t)
             first_product(1, t)
             ht = tile("h%d" % t, [P, S], F32)
             nc.scalar.activation(ht[:], acc[t][:], ACT.Silu)

@@ -40,7 +40,6 @@ def tile_picked_pna_silu_p_kernel(
         nc.scalar.activation(warm[:], warm_in[:], ACT.Silu)
 
         offs_sb = tile("offs_sb", [P, S // 16], U16)
-        nc.sync.dma_start(offs_sb[:], offs)
 
         xs_all = tile("xs_all", [P, T], U8)
         nc.vector.memset(xs_all[:].bitcast(I32), 0)
@@ -49,6 +48,7 @@ def tile_picked_pna_silu_p_kernel(
 
         xw_all = [tile("xw_all%d" % z, [P, T], U32) for z in range(PASSES)]
         nc.sync.dma_start(xw_all[0][:].bitcast(I32), x_words[0].rearrange("p n t -> p (n t)").bitcast(I32))
+        nc.sync.dma_start(offs_sb[:], offs)
         for q in range(4):
             nc.sync.dma_start(
                 xs_all[32 * q : 32 * q + 4 * PASSES, :].bitcast(I32),
@@ -104,16 +104,16 @@ def tile_picked_pna_silu_p_kernel(
                 in_=wb[z, u][:, e0:e1, :, :].rearrange("p e m j -> p (e m j)"),
             )
 
-        acc = [ps.tile([P, S], F32, name="acc%d" % t) for t in range(PACK)]
+        spans = [(0, 0, S // 2), (0, S // 2, S)] + [(t, 0, S) for t in range(1, PACK)]
 
-        def first_product(z, t):
+        def first_product(z, t, acc, c0, c1):
             u, e = divmod(t, 2)
             nc.tensor.matmul_mx(
-                out=acc[t][:],
+                out=acc[:],
                 lhsT=wc[z, u][:, e * P : (e + 1) * P].bitcast(FP8X4),
                 lhsT_scale=wsc[z, u][:, e * P : (e + 1) * P],
-                rhs=xw[z][:].bitcast(FP8X4),
-                rhs_scale=xs[4 * z :, :],
+                rhs=xw[z][:, c0:c1].bitcast(FP8X4),
+                rhs_scale=xs[4 * z :, c0:c1],
                 start=(z == 0),
                 stop=(z == PASSES - 1),
             )
@@ -133,44 +133,43 @@ def tile_picked_pna_silu_p_kernel(
         quantise_w1(1, 0, 1, 2)
         quantise_w1(1, 1, 0, 2)
 
-        h = []
-        for t in range(PACK):
-            first_product(0, t)
-            first_product(1, t)
-            ht = tile("h%d" % t, [P, S], F32)
-            nc.scalar.activation(ht[:], acc[t][:], ACT.Silu)
-            h.append(ht)
+        h = [tile("h%d" % t, [P, S], F32) for t in range(PACK)]
+        for i, (t, c0, c1) in enumerate(spans):
+            acc = ps.tile([P, c1 - c0], F32, name="acc%d" % i, tag="bank%d" % i)
+            first_product(0, t, acc, c0, c1)
+            first_product(1, t, acc, c0, c1)
+            nc.scalar.activation(h[t][:, c0:c1], acc[:], ACT.Silu)
 
         big01 = tile("big01", [P, 2, 2 * V], BF16)
         small01 = tile("small01", [P, 2, 2 * V], BF16)
-        last = tile("last", [P, 2, 2 * V], BF16)
-        back = ps.tile([P, 2, V], F32, name="back")
+        gb = [tile("gb%d" % d, [P, 2, 2 * V], BF16) for d in range(D)]
+        last = gb[2]
+        back = [ps.tile([P, 2, P], F32, name="back%d" % half, tag="bank%d" % (2, 7)[half]) for half in range(2)]
         for u in range(2):
             g = [tile("g%d_%d" % (u, d), [P, 2, V], F32) for d in range(D)]
-            total = ps.tile([P, 2, 2, P], F32, name="total%d" % u)
+            total = [
+                ps.tile([P, 2, P], F32, name="total%d_%d" % (u, half), tag="bank%d" % ((5, 0)[u] + half))
+                for half in range(2)
+            ]
             for e in range(2):
                 for d in range(D):
                     nc.vector.tensor_copy(g[d][:, e, :], h[2 * u + e][:].indirect(pos_sb[d][:]))
-                for half in range(2):
-                    for d in range(D):
+                    for half in range(2):
                         nc.tensor.matmul(
-                            total[:, half, e, :], lhsT=g[d][:, e, half * P : (half + 1) * P], rhs=ident[:],
+                            total[half][:, e, :], lhsT=g[d][:, e, half * P : (half + 1) * P], rhs=ident[:],
                             is_transpose=True, start=(d == 0), stop=(d == D - 1),
                         )
-            gb = [tile("gb%d_%d" % (u, d), [P, 2 * V], BF16) for d in range(D - 1)]
-            for d, dst in enumerate((gb[0][:], gb[1][:], last[:, u, :])):
-                nc.scalar.copy(dst.rearrange("p (v e) -> p v e", e=2), g[d][:].rearrange("p e v -> p v e"))
-            nc.vector.tensor_tensor(big01[:, u, :], gb[0][:], gb[1][:], ALU.max)
-            nc.vector.tensor_tensor(small01[:, u, :], gb[0][:], gb[1][:], ALU.min)
-            mean_t = tile("mean_t%d" % u, [P, 2, P, 2], BF16)
-            nc.scalar.activation(mean_t[:], total[:].rearrange("v h e p -> v h p e"), ACT.Copy, scale=1.0 / D)
+            for d in range(D):
+                nc.scalar.copy(gb[d][:, u, :].rearrange("p (v e) -> p v e", e=2), g[d][:].rearrange("p e v -> p v e"))
             for half in range(2):
+                mean_t = tile("mean_t%d_%d" % (u, half), [P, P, 2], BF16)
+                nc.scalar.activation(mean_t[:], total[half][:].rearrange("v e p -> v p e"), ACT.Copy, scale=1.0 / D)
                 nc.tensor.transpose(
-                    back[:, u, half * P : (half + 1) * P],
-                    mean_t[:, half, :, :].rearrange("v p e -> v (p e)").bitcast(F32),
-                    ident[:],
+                    back[half][:, u, :], mean_t[:].rearrange("v p e -> v (p e)").bitcast(F32), ident[:]
                 )
 
+        nc.vector.tensor_tensor(big01[:], gb[0][:], gb[1][:], ALU.max)
+        nc.vector.tensor_tensor(small01[:], gb[0][:], gb[1][:], ALU.min)
         zb = [tile("zb%d" % a, [P, PACK * V], BF16) for a in range(D)]
         for a, part, op in ((1, big01, ALU.max), (2, small01, ALU.min)):
             nc.vector.tensor_tensor(
@@ -179,18 +178,34 @@ def tile_picked_pna_silu_p_kernel(
                 last[:].rearrange("p u (v e) -> p v u e", e=2),
                 op,
             )
-        nc.scalar.copy(zb[0][:].bitcast(F32).rearrange("p (v u) -> p v u", u=2), back[:].rearrange("p u v -> p v u"))
-
-        res = ps.tile([P, V], F32, name="res")
-        order = (1, 2, 0)
-        for i, a in enumerate(order):
-            zc = tile("zc%d" % a, [P, V], U32)
-            zs = tile("zs%d" % a, [P, V], U8)
-            nc.vector.quantize_mx(out=zc[:].bitcast(FP8X4), scales=zs[:], in_=zb[a][:])
-            nc.tensor.matmul_mx(
-                out=res[:], lhsT=ww[a][:].bitcast(FP8X4), lhsT_scale=ws_all[:, a * N : (a + 1) * N],
-                rhs=zc[:].bitcast(FP8X4), rhs_scale=zs[:], start=(i == 0), stop=(i == D - 1),
+        for half in range(2):
+            nc.scalar.copy(
+                zb[0][:, half * P * PACK : (half + 1) * P * PACK].bitcast(F32).rearrange("p (v u) -> p v u", u=2),
+                back[half][:].rearrange("p u v -> p v u"),
             )
-        res_sb = tile("res_sb", [P, V], F32)
-        nc.scalar.copy(res_sb[:], res[:])
-        nc.sync.dma_start(out, res_sb[:])
+
+        zc = [tile("zc%d" % a, [P, V], U32) for a in range(D)]
+        zs = [tile("zs%d" % a, [P, V], U8) for a in range(D)]
+        res = [ps.tile([P, P], F32, name="res%d" % half, tag="bank%d" % (3 + half)) for half in range(2)]
+
+        def second_product(a, half, start, stop):
+            cols = slice(half * P, (half + 1) * P)
+            nc.tensor.matmul_mx(
+                out=res[half][:], lhsT=ww[a][:].bitcast(FP8X4), lhsT_scale=ws_all[:, a * N : (a + 1) * N],
+                rhs=zc[a][:, cols].bitcast(FP8X4), rhs_scale=zs[a][:, cols], start=start, stop=stop,
+            )
+
+        for a in (1, 2):
+            nc.vector.quantize_mx(out=zc[a][:].bitcast(FP8X4), scales=zs[a][:], in_=zb[a][:])
+            for half in range(2):
+                second_product(a, half, a == 1, False)
+        for half, copy in ((0, nc.scalar.copy), (1, nc.vector.tensor_copy)):
+            cols = slice(half * P, (half + 1) * P)
+            nc.vector.quantize_mx(
+                out=zc[0][:, cols].bitcast(FP8X4), scales=zs[0][:, cols],
+                in_=zb[0][:, half * P * PACK : (half + 1) * P * PACK],
+            )
+            second_product(0, half, False, True)
+            res_sb = tile("res_sb%d" % half, [P, P], F32)
+            copy(res_sb[:], res[half][:])
+            nc.sync.dma_start(out[:, cols], res_sb[:])

@@ -54,7 +54,7 @@ def tile_picked_pna_silu_p_kernel(
                 xs_all[32 * q : 32 * q + 4 * PASSES, :].bitcast(I32),
                 x_scales[:, 4 * q : 4 * q + 4, :].bitcast(I32),
             )
-        pieces = [(0, 0, H), (1, 0, H // 2), (1, H // 2, H)]
+        pieces = [(0, 0, H), (1, 0, H)]
         w1_raw = []
         for z, c0, c1 in pieces:
             raw = tile("w1_raw%d_%d" % (z, c0), [P, PACK, c1 - c0], F32)
@@ -118,17 +118,17 @@ def tile_picked_pna_silu_p_kernel(
                 stop=(z == PASSES - 1),
             )
 
-        for (z, c0, c1), raw in zip(pieces, w1_raw):
-            src = raw[:].rearrange("p j (m t) -> p m j t", t=PACK)
-            for u, copy in ((0, nc.vector.tensor_copy), (1, nc.scalar.copy)):
-                copy(
-                    wb[z, u][:, :, c0 // PACK : c1 // PACK, :].rearrange("p e m j -> p m j e"),
-                    src[:, :, :, 2 * u : 2 * u + 2],
-                )
-            if z == 0:
-                quantise_w1(0, 0, 0, 2)
-                nc.vector.tensor_copy(xw[1][:], xw_all[1][:].indirect(offs_sb[:]))
-                quantise_w1(0, 1, 0, 2)
+        def round_w1(copy, z, u, m0, m1):
+            src = w1_raw[z][:].rearrange("p j (m t) -> p m j t", t=PACK)
+            copy(wb[z, u][:, :, m0:m1, :].rearrange("p e m j -> p m j e"), src[:, m0:m1, :, 2 * u : 2 * u + 2])
+
+        round_w1(nc.vector.tensor_copy, 0, 0, 0, P)
+        round_w1(nc.scalar.copy, 0, 1, 0, P)
+        quantise_w1(0, 0, 0, 2)
+        nc.vector.tensor_copy(xw[1][:], xw_all[1][:].indirect(offs_sb[:]))
+        quantise_w1(0, 1, 0, 2)
+        round_w1(nc.vector.tensor_copy, 1, 0, 0, P)
+        round_w1(nc.scalar.copy, 1, 1, 0, P)
         quantise_w1(1, 0, 0, 1)
         quantise_w1(1, 0, 1, 2)
         quantise_w1(1, 1, 0, 2)
@@ -161,6 +161,8 @@ def tile_picked_pna_silu_p_kernel(
                         )
             for d in range(D):
                 nc.scalar.copy(gb[d][:, u, :].rearrange("p (v e) -> p v e", e=2), g[d][:].rearrange("p e v -> p v e"))
+            nc.vector.tensor_tensor(big01[:, u, :], gb[0][:, u, :], gb[1][:, u, :], ALU.max)
+            nc.vector.tensor_tensor(small01[:, u, :], gb[0][:, u, :], gb[1][:, u, :], ALU.min)
             for half in range(2):
                 mean_t = tile("mean_t%d_%d" % (u, half), [P, P, 2], BF16)
                 nc.scalar.activation(mean_t[:], total[half][:].rearrange("v e p -> v p e"), ACT.Copy, scale=1.0 / D)
@@ -168,8 +170,6 @@ def tile_picked_pna_silu_p_kernel(
                     back[half][:, u, :], mean_t[:].rearrange("v p e -> v (p e)").bitcast(F32), ident[:]
                 )
 
-        nc.vector.tensor_tensor(big01[:], gb[0][:], gb[1][:], ALU.max)
-        nc.vector.tensor_tensor(small01[:], gb[0][:], gb[1][:], ALU.min)
         zb = [tile("zb%d" % a, [P, PACK * V], BF16) for a in range(D)]
         for a, part, op in ((1, big01, ALU.max), (2, small01, ALU.min)):
             nc.vector.tensor_tensor(

@@ -31,8 +31,8 @@ def tile_picked_pna_silu_p_kernel(
         sb = ctx.enter_context(tc.tile_pool(name="sb", bufs=1))
         ps = ctx.enter_context(tc.psum_pool(name="ps", bufs=1))
 
-        def tile(name, shape, dtype):
-            return sb.tile(shape, dtype, name=name, align_bytes=64)
+        def tile(name, shape, dtype, tag=None):
+            return sb.tile(shape, dtype, name=name, tag=tag or name, align_bytes=64)
 
         warm_in = tile("warm_in", [P, 8], F32)
         warm = tile("warm", [P, 8], F32)
@@ -140,42 +140,87 @@ def tile_picked_pna_silu_p_kernel(
             first_product(1, t, acc, c0, c1)
             nc.scalar.activation(h[t][:, c0:c1], acc[:], ACT.Silu)
 
-        big01 = tile("big01", [P, 2, 2 * V], BF16)
-        small01 = tile("small01", [P, 2, 2 * V], BF16)
-        gb = [tile("gb%d" % d, [P, 2, 2 * V], BF16) for d in range(D)]
-        last = gb[2]
-        back = [ps.tile([P, 2, P], F32, name="back%d" % half, tag="bank%d" % (2, 7)[half]) for half in range(2)]
-        for u in range(2):
-            g = [tile("g%d_%d" % (u, d), [P, 2, V], F32) for d in range(D)]
-            total = [
-                ps.tile([P, 2, P], F32, name="total%d_%d" % (u, half), tag="bank%d" % ((5, 0)[u] + half))
-                for half in range(2)
-            ]
-            for e in range(2):
-                for d in range(D):
-                    nc.vector.tensor_copy(g[d][:, e, :], h[2 * u + e][:].indirect(pos_sb[d][:]))
-                    for half in range(2):
-                        nc.tensor.matmul(
-                            total[half][:, e, :], lhsT=g[d][:, e, half * P : (half + 1) * P], rhs=ident[:],
-                            is_transpose=True, start=(d == 0), stop=(d == D - 1),
-                        )
-            for d in range(D):
-                nc.scalar.copy(gb[d][:, u, :].rearrange("p (v e) -> p v e", e=2), g[d][:].rearrange("p e v -> p v e"))
-            nc.vector.tensor_tensor(big01[:, u, :], gb[0][:, u, :], gb[1][:, u, :], ALU.max)
-            nc.vector.tensor_tensor(small01[:, u, :], gb[0][:, u, :], gb[1][:, u, :], ALU.min)
+        g = [
+            [tile("g%d_%d" % (u, d), [P, 2, V], F32, tag="wc1_1" if (u, d) == (0, 0) else None) for d in range(D)]
+            for u in range(2)
+        ]
+        total = [ps.tile([P, 2, 2, P], F32, name="total%d" % u, tag="bank%d" % (5 + u)) for u in range(2)]
+        turned_so_far = [0, 0]
+
+        def add_turned(t, d):
+            u, e = divmod(t, 2)
             for half in range(2):
-                mean_t = tile("mean_t%d_%d" % (u, half), [P, P, 2], BF16)
-                nc.scalar.activation(mean_t[:], total[half][:].rearrange("v e p -> v p e"), ACT.Copy, scale=1.0 / D)
-                nc.tensor.transpose(
-                    back[half][:, u, :], mean_t[:].rearrange("v p e -> v (p e)").bitcast(F32), ident[:]
+                nc.tensor.matmul(
+                    total[u][:, half, e, :], lhsT=g[u][d][:, e, half * P : (half + 1) * P], rhs=ident[:],
+                    is_transpose=True, start=(turned_so_far[u] == 0), stop=(turned_so_far[u] == 4 * D - 1),
                 )
+                turned_so_far[u] = turned_so_far[u] + 1
+
+        def gather_vector(t, d):
+            nc.vector.tensor_copy(g[t // 2][d][:, t % 2, :], h[t][:].indirect(pos_sb[d][:]))
+            add_turned(t, d)
+
+        def gather_scalar(t, d):
+            nc.scalar.activation(g[t // 2][d][:, t % 2, :], h[t][:].indirect(pos_sb[d][:]), ACT.Copy)
+            add_turned(t, d)
+
+        big = tile("big", [P, 2, 2 * V], BF16)
+        small = tile("small", [P, 2, 2 * V], BF16)
+        first = tile("first", [P, 2, 2 * V], BF16)
+        gb = {(u, d): tile("gb%d_%d" % (u, d), [P, 2 * V], BF16) for u in range(2) for d in (1, 2)}
+        back = [ps.tile([P, 2, P], F32, name="back%d" % half, tag="bank%d" % (2, 7)[half]) for half in range(2)]
+
+        def paired(ap):
+            return ap.rearrange("p (v e) -> p v e", e=2)
+
+        def turned(ap):
+            return ap.rearrange("p e v -> p v e")
+
+        def round_gpsimd(u, d):
+            nc.gpsimd.tensor_scalar(paired(gb[u, d][:]), turned(g[u][d][:]), 1.0, 0.0, ALU.mult, ALU.add)
+
+        def extremes(u):
+            nc.vector.tensor_tensor(big[:, u, :], gb[u, 1][:], gb[u, 2][:], ALU.max)
+            nc.vector.tensor_tensor(small[:, u, :], gb[u, 1][:], gb[u, 2][:], ALU.min)
+
+        def turn_back(u, half, mean_t):
+            nc.tensor.transpose(back[half][:, u, :], mean_t.rearrange("v p e -> v (p e)").bitcast(F32), ident[:])
+
+        gather_vector(0, 1)
+        gather_vector(0, 2)
+        gather_vector(1, 1)
+        round_gpsimd(0, 1)
+        gather_vector(1, 2)
+        round_gpsimd(0, 2)
+        gather_scalar(2, 1)
+        gather_vector(2, 2)
+        gather_scalar(3, 1)
+        round_gpsimd(1, 1)
+        gather_vector(2, 0)
+        gather_scalar(3, 0)
+        gather_vector(3, 2)
+        gather_scalar(0, 0)
+        gather_scalar(1, 0)
+        extremes(0)
+        nc.vector.tensor_copy(paired(gb[1, 2][:]), turned(g[1][2][:]))
+        nc.vector.tensor_copy(paired(first[:, 1, :]), turned(g[1][0][:]))
+        extremes(1)
+        mean1 = tile("mean1", [P, 2, P, 2], BF16)
+        nc.scalar.activation(mean1[:], total[1][:].rearrange("v h e p -> v h p e"), ACT.Copy, scale=1.0 / D)
+        for half in range(2):
+            turn_back(1, half, mean1[:, half, :, :])
+        nc.scalar.copy(paired(first[:, 0, :]), turned(g[0][0][:]))
+        for half in range(2):
+            mean0 = tile("mean0_%d" % half, [P, P, 2], BF16)
+            nc.scalar.activation(mean0[:], total[0][:, half, :, :].rearrange("v e p -> v p e"), ACT.Copy, scale=1.0 / D)
+            turn_back(0, half, mean0[:])
 
         zb = [tile("zb%d" % a, [P, PACK * V], BF16) for a in range(D)]
-        for a, part, op in ((1, big01, ALU.max), (2, small01, ALU.min)):
+        for a, part, op in ((1, big, ALU.max), (2, small, ALU.min)):
             nc.vector.tensor_tensor(
                 zb[a][:].rearrange("p (v u e) -> p v u e", u=2, e=2),
                 part[:].rearrange("p u (v e) -> p v u e", e=2),
-                last[:].rearrange("p u (v e) -> p v u e", e=2),
+                first[:].rearrange("p u (v e) -> p v u e", e=2),
                 op,
             )
         for half in range(2):

@@ -125,49 +125,61 @@ def tile_picked_pna_silu_p_kernel(
         round_w1(nc.vector.tensor_copy, 0, 0, 0, P)
         round_w1(nc.scalar.copy, 0, 1, 0, P)
         quantise_w1(0, 0, 0, 2)
-        nc.vector.tensor_copy(xw[1][:], xw_all[1][:].indirect(offs_sb[:]))
         quantise_w1(0, 1, 0, 2)
-        round_w1(nc.vector.tensor_copy, 1, 0, 0, P)
-        round_w1(nc.scalar.copy, 1, 1, 0, P)
+        nc.vector.tensor_copy(xw[1][:], xw_all[1][:].indirect(offs_sb[:]))
+        round_w1(nc.vector.tensor_copy, 1, 0, 0, 72)
+        round_w1(nc.scalar.copy, 1, 0, 72, P)
+        round_w1(nc.vector.tensor_copy, 1, 1, 0, 64)
         quantise_w1(1, 0, 0, 1)
         quantise_w1(1, 0, 1, 2)
+        round_w1(nc.scalar.copy, 1, 1, 64, P)
         quantise_w1(1, 1, 0, 2)
 
         h = [tile("h%d" % t, [P, S], F32) for t in range(PACK)]
+        accs = []
         for i, (t, c0, c1) in enumerate(spans):
             acc = ps.tile([P, c1 - c0], F32, name="acc%d" % i, tag="bank%d" % i)
             first_product(0, t, acc, c0, c1)
             first_product(1, t, acc, c0, c1)
-            nc.scalar.activation(h[t][:, c0:c1], acc[:], ACT.Silu)
+            accs.append(acc)
+
+        def silu(t):
+            for acc, (tt, c0, c1) in zip(accs, spans):
+                if tt == t:
+                    nc.scalar.activation(h[t][:, c0:c1], acc[:], ACT.Silu)
 
         g = [
-            [tile("g%d_%d" % (u, d), [P, 2, V], F32, tag="wc1_1" if (u, d) == (0, 0) else None) for d in range(D)]
+            [tile("g%d_%d" % (u, d), [P, 2, V], F32) for d in range(D)]
             for u in range(2)
         ]
         total = [ps.tile([P, 2, 2, P], F32, name="total%d" % u, tag="bank%d" % (5 + u)) for u in range(2)]
         turned_so_far = [0, 0]
 
-        def add_turned(t, d):
+        def add_turned(t, d, halves):
             u, e = divmod(t, 2)
-            for half in range(2):
+            for half in halves:
                 nc.tensor.matmul(
                     total[u][:, half, e, :], lhsT=g[u][d][:, e, half * P : (half + 1) * P], rhs=ident[:],
                     is_transpose=True, start=(turned_so_far[u] == 0), stop=(turned_so_far[u] == 4 * D - 1),
                 )
                 turned_so_far[u] = turned_so_far[u] + 1
 
-        def gather_vector(t, d):
-            nc.vector.tensor_copy(g[t // 2][d][:, t % 2, :], h[t][:].indirect(pos_sb[d][:]))
-            add_turned(t, d)
+        def gather_vector(t, d, halves=(0, 1)):
+            v0, v1 = halves[0] * P, (halves[-1] + 1) * P
+            nc.vector.tensor_copy(g[t // 2][d][:, t % 2, v0:v1], h[t][:].indirect(pos_sb[d][:, v0 // 16 : v1 // 16]))
+            add_turned(t, d, halves)
 
-        def gather_scalar(t, d):
-            nc.scalar.activation(g[t // 2][d][:, t % 2, :], h[t][:].indirect(pos_sb[d][:]), ACT.Copy)
-            add_turned(t, d)
+        def gather_scalar(t, d, halves=(0, 1)):
+            v0, v1 = halves[0] * P, (halves[-1] + 1) * P
+            nc.scalar.activation(
+                g[t // 2][d][:, t % 2, v0:v1], h[t][:].indirect(pos_sb[d][:, v0 // 16 : v1 // 16]), ACT.Copy
+            )
+            add_turned(t, d, halves)
 
         big = tile("big", [P, 2, 2 * V], BF16)
         small = tile("small", [P, 2, 2 * V], BF16)
         first = tile("first", [P, 2, 2 * V], BF16)
-        gb = {(u, d): tile("gb%d_%d" % (u, d), [P, 2 * V], BF16) for u in range(2) for d in (1, 2)}
+        gb = {(u, d): tile("gb%d_%d" % (u, d), [P, 2 * V], BF16) for u in range(1) for d in (1, 2)}
         back = [ps.tile([P, 2, P], F32, name="back%d" % half, tag="bank%d" % (2, 7)[half]) for half in range(2)]
 
         def paired(ap):
@@ -176,8 +188,14 @@ def tile_picked_pna_silu_p_kernel(
         def turned(ap):
             return ap.rearrange("p e v -> p v e")
 
+        def rounded(u, d):
+            return first[:, u, :] if d == 0 else gb[u, d][:]
+
         def round_gpsimd(u, d):
-            nc.gpsimd.tensor_scalar(paired(gb[u, d][:]), turned(g[u][d][:]), 1.0, 0.0, ALU.mult, ALU.add)
+            nc.gpsimd.tensor_scalar(paired(rounded(u, d)), turned(g[u][d][:]), 1.0, 0.0, ALU.mult, ALU.add)
+
+        def round_with(copy, u, d):
+            copy(paired(rounded(u, d)), turned(g[u][d][:]))
 
         def extremes(u):
             nc.vector.tensor_tensor(big[:, u, :], gb[u, 1][:], gb[u, 2][:], ALU.max)
@@ -186,34 +204,38 @@ def tile_picked_pna_silu_p_kernel(
         def turn_back(u, half, mean_t):
             nc.tensor.transpose(back[half][:, u, :], mean_t.rearrange("v p e -> v (p e)").bitcast(F32), ident[:])
 
+        silu(0)
         gather_vector(0, 1)
-        gather_vector(0, 2)
+        silu(1)
+        gather_scalar(0, 0)
         gather_vector(1, 1)
         round_gpsimd(0, 1)
+        silu(2)
+        gather_scalar(0, 2)
+        gather_vector(1, 0)
+        round_gpsimd(0, 0)
         gather_vector(1, 2)
         round_gpsimd(0, 2)
-        gather_scalar(2, 1)
-        gather_vector(2, 2)
-        gather_scalar(3, 1)
-        round_gpsimd(1, 1)
-        gather_vector(2, 0)
+        silu(3)
+        gather_vector(2, 1)
+        gather_scalar(2, 0)
+        gather_vector(3, 1)
+        gather_scalar(2, 2)
+        gather_vector(3, 2, (0,))
+        gather_scalar(3, 2, (1,))
         gather_scalar(3, 0)
-        gather_vector(3, 2)
-        gather_scalar(0, 0)
-        gather_scalar(1, 0)
         extremes(0)
-        nc.vector.tensor_copy(paired(gb[1, 2][:]), turned(g[1][2][:]))
-        nc.vector.tensor_copy(paired(first[:, 1, :]), turned(g[1][0][:]))
-        extremes(1)
-        mean1 = tile("mean1", [P, 2, P, 2], BF16)
-        nc.scalar.activation(mean1[:], total[1][:].rearrange("v h e p -> v h p e"), ACT.Copy, scale=1.0 / D)
+        nc.vector.tensor_tensor(paired(big[:, 1, :]), turned(g[1][1][:]), turned(g[1][2][:]), ALU.max)
+        nc.vector.tensor_tensor(paired(small[:, 1, :]), turned(g[1][1][:]), turned(g[1][2][:]), ALU.min)
+        round_with(nc.scalar.copy, 1, 0)
+        mean0 = tile("mean0", [P, 2, P, 2], BF16)
+        nc.scalar.activation(mean0[:], total[0][:].rearrange("v h e p -> v h p e"), ACT.Copy, scale=1.0 / D)
         for half in range(2):
-            turn_back(1, half, mean1[:, half, :, :])
-        nc.scalar.copy(paired(first[:, 0, :]), turned(g[0][0][:]))
+            turn_back(0, half, mean0[:, half, :, :])
         for half in range(2):
-            mean0 = tile("mean0_%d" % half, [P, P, 2], BF16)
-            nc.scalar.activation(mean0[:], total[0][:, half, :, :].rearrange("v e p -> v p e"), ACT.Copy, scale=1.0 / D)
-            turn_back(0, half, mean0[:])
+            mean1 = tile("mean1_%d" % half, [P, P, 2], BF16)
+            nc.scalar.activation(mean1[:], total[1][:, half, :, :].rearrange("v e p -> v p e"), ACT.Copy, scale=1.0 / D)
+            turn_back(1, half, mean1[:])
 
         zb = [tile("zb%d" % a, [P, PACK * V], BF16) for a in range(D)]
         for a, part, op in ((1, big, ALU.max), (2, small, ALU.min)):

@@ -54,7 +54,7 @@ def tile_picked_pna_silu_p_kernel(
                 xs_all[32 * q : 32 * q + 4 * PASSES, :].bitcast(I32),
                 x_scales[:, 4 * q : 4 * q + 4, :].bitcast(I32),
             )
-        pieces = [(0, 0, H), (1, 0, H)]
+        pieces = [(0, 0, H), (1, 0, H // 2), (1, H // 2, H)]
         w1_raw = []
         for z, c0, c1 in pieces:
             raw = tile("w1_raw%d_%d" % (z, c0), [P, PACK, c1 - c0], F32)
@@ -119,19 +119,34 @@ def tile_picked_pna_silu_p_kernel(
             )
 
         def round_w1(copy, z, u, m0, m1):
-            src = w1_raw[z][:].rearrange("p j (m t) -> p m j t", t=PACK)
-            copy(wb[z, u][:, :, m0:m1, :].rearrange("p e m j -> p m j e"), src[:, m0:m1, :, 2 * u : 2 * u + 2])
+            piece, first_m = (0, 0) if z == 0 else ((1, 0) if m0 < P // 2 else (2, P // 2))
+            src = w1_raw[piece][:].rearrange("p j (m t) -> p m j t", t=PACK)
+            copy(
+                wb[z, u][:, :, m0:m1, :].rearrange("p e m j -> p m j e"),
+                src[:, m0 - first_m : m1 - first_m, :, 2 * u : 2 * u + 2],
+            )
+
+        def quantise_half(t, half):
+            u, e = divmod(t, 2)
+            c0 = e * P + half * P // 2
+            nc.vector.quantize_mx(
+                out=wc[1, u][:, c0 : c0 + P // 2].bitcast(FP8X4),
+                scales=wsc[1, u][:, c0 : c0 + P // 2],
+                in_=wb[1, u][:, e, half * P // 2 : (half + 1) * P // 2, :].rearrange("p m j -> p (m j)"),
+            )
 
         round_w1(nc.vector.tensor_copy, 0, 0, 0, P)
         round_w1(nc.scalar.copy, 0, 1, 0, P)
         quantise_w1(0, 0, 0, 2)
         quantise_w1(0, 1, 0, 2)
         nc.vector.tensor_copy(xw[1][:], xw_all[1][:].indirect(offs_sb[:]))
-        round_w1(nc.vector.tensor_copy, 1, 0, 0, 72)
-        round_w1(nc.scalar.copy, 1, 0, 72, P)
-        round_w1(nc.vector.tensor_copy, 1, 1, 0, 64)
-        quantise_w1(1, 0, 0, 1)
-        quantise_w1(1, 0, 1, 2)
+        round_w1(nc.scalar.copy, 1, 0, 0, 64)
+        round_w1(nc.scalar.copy, 1, 1, 0, 64)
+        round_w1(nc.vector.tensor_copy, 1, 0, 64, P)
+        quantise_half(0, 0)
+        quantise_half(1, 0)
+        quantise_half(0, 1)
+        quantise_half(1, 1)
         round_w1(nc.scalar.copy, 1, 1, 64, P)
         quantise_w1(1, 1, 0, 2)
 

@@ -18,8 +18,12 @@ ALU = mybir.AluOpType
 
 P = 128
 PACK = 4
-PASSES = K // (P * PACK)
+K_PASS = P * PACK
+PASSES = K // K_PASS
+QUADRANTS = 4
 D = 3
+LIST_ROWS = 16
+HALF_M = P // 2
 
 
 def tile_picked_pna_silu_p_kernel(
@@ -31,50 +35,56 @@ def tile_picked_pna_silu_p_kernel(
         sb = ctx.enter_context(tc.tile_pool(name="sb", bufs=1))
         ps = ctx.enter_context(tc.psum_pool(name="ps", bufs=1))
 
-        def tile(name, shape, dtype, tag=None):
-            return sb.tile(shape, dtype, name=name, tag=tag or name, align_bytes=64)
+        def tile(name, shape, dtype):
+            return sb.tile(shape, dtype, name=name, align_bytes=64)
+
+        def bank(name, shape, number):
+            return ps.tile(shape, F32, name=name, tag="bank%d" % number)
 
         warm_in = tile("warm_in", [P, 8], F32)
         warm = tile("warm", [P, 8], F32)
         nc.gpsimd.memset(warm_in[:], 0.0)
         nc.scalar.activation(warm[:], warm_in[:], ACT.Silu)
 
-        offs_sb = tile("offs_sb", [P, S // 16], U16)
+        offs_sb = tile("offs_sb", [P, S // LIST_ROWS], U16)
 
         xs_all = tile("xs_all", [P, T], U8)
         nc.vector.memset(xs_all[:].bitcast(I32), 0)
         ws_all = tile("ws_all", [P, D * N], U8)
         nc.vector.memset(ws_all[:].bitcast(I32), 0)
 
+        def load_words(dst, words):
+            nc.sync.dma_start(dst[:].bitcast(I32), words.rearrange("p n t -> p (n t)").bitcast(I32))
+
+        def load_w1(z, c0, c1):
+            raw = tile("w1_raw%d_%d" % (z, c0), [P, PACK, c1 - c0], F32)
+            nc.sync.dma_start(raw[:], w1[K_PASS * z : K_PASS * (z + 1), c0:c1].rearrange("(p j) c -> p j c", j=PACK))
+            return raw
+
         xw_all = [tile("xw_all%d" % z, [P, T], U32) for z in range(PASSES)]
-        nc.sync.dma_start(xw_all[0][:].bitcast(I32), x_words[0].rearrange("p n t -> p (n t)").bitcast(I32))
+        load_words(xw_all[0], x_words[0])
         nc.sync.dma_start(offs_sb[:], offs)
-        for q in range(4):
+        for q in range(QUADRANTS):
             nc.sync.dma_start(
                 xs_all[32 * q : 32 * q + 4 * PASSES, :].bitcast(I32),
                 x_scales[:, 4 * q : 4 * q + 4, :].bitcast(I32),
             )
-        pieces = [(0, 0, H), (1, 0, H // 2), (1, H // 2, H)]
-        w1_raw = []
-        for z, c0, c1 in pieces:
-            raw = tile("w1_raw%d_%d" % (z, c0), [P, PACK, c1 - c0], F32)
-            nc.sync.dma_start(raw[:], w1[512 * z : 512 * (z + 1), c0:c1].rearrange("(p j) c -> p j c", j=PACK))
-            w1_raw.append(raw)
-            if z == 0:
-                nc.sync.dma_start(xw_all[1][:].bitcast(I32), x_words[1].rearrange("p n t -> p (n t)").bitcast(I32))
+        w1_first = load_w1(0, 0, H)
+        load_words(xw_all[1], x_words[1])
+        w1_last = [load_w1(1, 0, H // 2), load_w1(1, H // 2, H)]
 
         pos_sb = []
         for d, pos in enumerate((pos1, pos2, pos3)):
-            lst = tile("pos_sb%d" % d, [P, V // 16], U16)
+            lst = tile("pos_sb%d" % d, [P, V // LIST_ROWS], U16)
             nc.sync.dma_start(lst[:], pos)
             pos_sb.append(lst)
 
         ww = []
         for a, (words, scales) in enumerate(((w2_words, w2_scales), (w3_words, w3_scales), (w4_words, w4_scales))):
             wt = tile("ww%d" % a, [P, N], U32)
-            nc.sync.dma_start(wt[:].bitcast(I32), words[0].rearrange("p n t -> p (n t)").bitcast(I32))
+            load_words(wt, words[0])
             ww.append(wt)
-            for q in range(4):
+            for q in range(QUADRANTS):
                 nc.sync.dma_start(
                     ws_all[32 * q : 32 * q + 4, a * N : (a + 1) * N].bitcast(I32),
                     scales[0, 4 * q : 4 * q + 4, :].bitcast(I32),
@@ -97,152 +107,123 @@ def tile_picked_pna_silu_p_kernel(
                 wc[z, u] = tile("wc%d_%d" % (z, u), [P, 2 * P], U32)
                 wsc[z, u] = tile("wsc%d_%d" % (z, u), [P, 2 * P], U8)
 
-        def quantise_w1(z, u, e0, e1):
-            nc.vector.quantize_mx(
-                out=wc[z, u][:, e0 * P : e1 * P].bitcast(FP8X4),
-                scales=wsc[z, u][:, e0 * P : e1 * P],
-                in_=wb[z, u][:, e0:e1, :, :].rearrange("p e m j -> p (e m j)"),
-            )
-
-        spans = [(0, 0, S // 2), (0, S // 2, S)] + [(t, 0, S) for t in range(1, PACK)]
-
-        def first_product(z, t, acc, c0, c1):
-            u, e = divmod(t, 2)
-            nc.tensor.matmul_mx(
-                out=acc[:],
-                lhsT=wc[z, u][:, e * P : (e + 1) * P].bitcast(FP8X4),
-                lhsT_scale=wsc[z, u][:, e * P : (e + 1) * P],
-                rhs=xw[z][:, c0:c1].bitcast(FP8X4),
-                rhs_scale=xs[4 * z :, c0:c1],
-                start=(z == 0),
-                stop=(z == PASSES - 1),
-            )
-
-        def round_w1(copy, z, u, m0, m1):
-            piece, first_m = (0, 0) if z == 0 else ((1, 0) if m0 < P // 2 else (2, P // 2))
-            src = w1_raw[piece][:].rearrange("p j (m t) -> p m j t", t=PACK)
+        def round_w1(copy, raw, z, u, m0, m1):
             copy(
                 wb[z, u][:, :, m0:m1, :].rearrange("p e m j -> p m j e"),
-                src[:, m0 - first_m : m1 - first_m, :, 2 * u : 2 * u + 2],
+                raw[:].rearrange("p j (m t) -> p m j t", t=PACK)[:, :, :, 2 * u : 2 * u + 2],
             )
 
-        def quantise_half(t, half):
-            u, e = divmod(t, 2)
-            c0 = e * P + half * P // 2
+        def quantise_w1(z, u, c0, c1):
             nc.vector.quantize_mx(
-                out=wc[1, u][:, c0 : c0 + P // 2].bitcast(FP8X4),
-                scales=wsc[1, u][:, c0 : c0 + P // 2],
-                in_=wb[1, u][:, e, half * P // 2 : (half + 1) * P // 2, :].rearrange("p m j -> p (m j)"),
+                out=wc[z, u][:, c0:c1].bitcast(FP8X4),
+                scales=wsc[z, u][:, c0:c1],
+                in_=wb[z, u][:].rearrange("p e m j -> p (e m j)")[:, c0 * PACK : c1 * PACK],
             )
 
-        round_w1(nc.vector.tensor_copy, 0, 0, 0, P)
-        round_w1(nc.scalar.copy, 0, 1, 0, P)
-        quantise_w1(0, 0, 0, 2)
-        quantise_w1(0, 1, 0, 2)
+        round_w1(nc.vector.tensor_copy, w1_first, 0, 0, 0, P)
+        round_w1(nc.scalar.copy, w1_first, 0, 1, 0, P)
+        for u in range(2):
+            quantise_w1(0, u, 0, 2 * P)
         nc.vector.tensor_copy(xw[1][:], xw_all[1][:].indirect(offs_sb[:]))
-        round_w1(nc.scalar.copy, 1, 0, 0, 64)
-        round_w1(nc.scalar.copy, 1, 1, 0, 64)
-        round_w1(nc.vector.tensor_copy, 1, 0, 64, P)
-        quantise_half(0, 0)
-        quantise_half(1, 0)
-        quantise_half(0, 1)
-        quantise_half(1, 1)
-        round_w1(nc.scalar.copy, 1, 1, 64, P)
-        quantise_w1(1, 1, 0, 2)
+        for u in range(2):
+            round_w1(nc.scalar.copy, w1_last[0], 1, u, 0, HALF_M)
+        round_w1(nc.vector.tensor_copy, w1_last[1], 1, 0, HALF_M, P)
+        for m0 in (0, HALF_M):
+            for e in range(2):
+                quantise_w1(1, 0, e * P + m0, e * P + m0 + HALF_M)
+        round_w1(nc.scalar.copy, w1_last[1], 1, 1, HALF_M, P)
+        quantise_w1(1, 1, 0, 2 * P)
 
+        spans = [(0, 0, S // 2), (0, S // 2, S)] + [(t, 0, S) for t in range(1, PACK)]
         h = [tile("h%d" % t, [P, S], F32) for t in range(PACK)]
         accs = []
         for i, (t, c0, c1) in enumerate(spans):
-            acc = ps.tile([P, c1 - c0], F32, name="acc%d" % i, tag="bank%d" % i)
-            first_product(0, t, acc, c0, c1)
-            first_product(1, t, acc, c0, c1)
+            u, e = divmod(t, 2)
+            acc = bank("acc%d" % i, [P, c1 - c0], i)
+            for z in range(PASSES):
+                nc.tensor.matmul_mx(
+                    out=acc[:],
+                    lhsT=wc[z, u][:, e * P : (e + 1) * P].bitcast(FP8X4),
+                    lhsT_scale=wsc[z, u][:, e * P : (e + 1) * P],
+                    rhs=xw[z][:, c0:c1].bitcast(FP8X4),
+                    rhs_scale=xs[4 * z :, c0:c1],
+                    start=(z == 0),
+                    stop=(z == PASSES - 1),
+                )
             accs.append(acc)
 
         def silu(t):
-            for acc, (tt, c0, c1) in zip(accs, spans):
-                if tt == t:
+            for acc, (tile_of_span, c0, c1) in zip(accs, spans):
+                if tile_of_span == t:
                     nc.scalar.activation(h[t][:, c0:c1], acc[:], ACT.Silu)
 
-        g = [
-            [tile("g%d_%d" % (u, d), [P, 2, V], F32) for d in range(D)]
-            for u in range(2)
-        ]
-        total = [ps.tile([P, 2, 2, P], F32, name="total%d" % u, tag="bank%d" % (5 + u)) for u in range(2)]
-        turned_so_far = [0, 0]
+        g = [[tile("g%d_%d" % (u, d), [P, 2, V], F32) for d in range(D)] for u in range(2)]
+
+        total = [bank("total%d" % u, [P, 2, 2, P], len(spans) + u) for u in range(2)]
+        added = [0, 0]
 
         def add_turned(t, d, halves):
             u, e = divmod(t, 2)
             for half in halves:
                 nc.tensor.matmul(
                     total[u][:, half, e, :], lhsT=g[u][d][:, e, half * P : (half + 1) * P], rhs=ident[:],
-                    is_transpose=True, start=(turned_so_far[u] == 0), stop=(turned_so_far[u] == 4 * D - 1),
+                    is_transpose=True, start=(added[u] == 0), stop=(added[u] == 4 * D - 1),
                 )
-                turned_so_far[u] = turned_so_far[u] + 1
+                added[u] = added[u] + 1
 
-        def gather_vector(t, d, halves=(0, 1)):
-            v0, v1 = halves[0] * P, (halves[-1] + 1) * P
-            nc.vector.tensor_copy(g[t // 2][d][:, t % 2, v0:v1], h[t][:].indirect(pos_sb[d][:, v0 // 16 : v1 // 16]))
-            add_turned(t, d, halves)
+        def scalar_copy(dst, src):
+            nc.scalar.activation(dst, src, ACT.Copy)
 
-        def gather_scalar(t, d, halves=(0, 1)):
+        def gather(copy, t, d, halves=(0, 1)):
             v0, v1 = halves[0] * P, (halves[-1] + 1) * P
-            nc.scalar.activation(
-                g[t // 2][d][:, t % 2, v0:v1], h[t][:].indirect(pos_sb[d][:, v0 // 16 : v1 // 16]), ACT.Copy
-            )
+            offsets = pos_sb[d][:, v0 // LIST_ROWS : v1 // LIST_ROWS]
+            copy(g[t // 2][d][:, t % 2, v0:v1], h[t][:].indirect(offsets))
             add_turned(t, d, halves)
 
         big = tile("big", [P, 2, 2 * V], BF16)
         small = tile("small", [P, 2, 2 * V], BF16)
         first = tile("first", [P, 2, 2 * V], BF16)
-        gb = {(u, d): tile("gb%d_%d" % (u, d), [P, 2 * V], BF16) for u in range(1) for d in (1, 2)}
-        back = [ps.tile([P, 2, P], F32, name="back%d" % half, tag="bank%d" % (2, 7)[half]) for half in range(2)]
+        second0 = tile("second0", [P, 2 * V], BF16)
+        third0 = tile("third0", [P, 2 * V], BF16)
+        back = [bank("back%d" % half, [P, 2, P], number) for half, number in enumerate((2, 7))]
 
         def paired(ap):
             return ap.rearrange("p (v e) -> p v e", e=2)
 
-        def turned(ap):
-            return ap.rearrange("p e v -> p v e")
+        def by_target(u, d):
+            return g[u][d][:].rearrange("p e v -> p v e")
 
-        def rounded(u, d):
-            return first[:, u, :] if d == 0 else gb[u, d][:]
+        def turn_back(u, half, mean_half):
+            nc.tensor.transpose(back[half][:, u, :], mean_half.rearrange("v p e -> v (p e)").bitcast(F32), ident[:])
 
-        def round_gpsimd(u, d):
-            nc.gpsimd.tensor_scalar(paired(rounded(u, d)), turned(g[u][d][:]), 1.0, 0.0, ALU.mult, ALU.add)
-
-        def round_with(copy, u, d):
-            copy(paired(rounded(u, d)), turned(g[u][d][:]))
-
-        def extremes(u):
-            nc.vector.tensor_tensor(big[:, u, :], gb[u, 1][:], gb[u, 2][:], ALU.max)
-            nc.vector.tensor_tensor(small[:, u, :], gb[u, 1][:], gb[u, 2][:], ALU.min)
-
-        def turn_back(u, half, mean_t):
-            nc.tensor.transpose(back[half][:, u, :], mean_t.rearrange("v p e -> v (p e)").bitcast(F32), ident[:])
-
+        on_vector, on_scalar = nc.vector.tensor_copy, scalar_copy
         silu(0)
-        gather_vector(0, 1)
+        gather(on_vector, 0, 1)
         silu(1)
-        gather_scalar(0, 0)
-        gather_vector(1, 1)
-        round_gpsimd(0, 1)
+        gather(on_scalar, 0, 0)
+        gather(on_vector, 1, 1)
+        nc.gpsimd.tensor_copy(paired(second0[:]), by_target(0, 1))
         silu(2)
-        gather_scalar(0, 2)
-        gather_vector(1, 0)
-        round_gpsimd(0, 0)
-        gather_vector(1, 2)
-        round_gpsimd(0, 2)
+        gather(on_scalar, 0, 2)
+        gather(on_vector, 1, 0)
+        nc.gpsimd.tensor_copy(paired(first[:, 0, :]), by_target(0, 0))
+        gather(on_vector, 1, 2)
+        nc.gpsimd.tensor_copy(paired(third0[:]), by_target(0, 2))
         silu(3)
-        gather_vector(2, 1)
-        gather_scalar(2, 0)
-        gather_vector(3, 1)
-        gather_scalar(2, 2)
-        gather_vector(3, 2, (0,))
-        gather_scalar(3, 2, (1,))
-        gather_scalar(3, 0)
-        extremes(0)
-        nc.vector.tensor_tensor(paired(big[:, 1, :]), turned(g[1][1][:]), turned(g[1][2][:]), ALU.max)
-        nc.vector.tensor_tensor(paired(small[:, 1, :]), turned(g[1][1][:]), turned(g[1][2][:]), ALU.min)
-        round_with(nc.scalar.copy, 1, 0)
+        gather(on_vector, 2, 1)
+        gather(on_scalar, 2, 0)
+        gather(on_vector, 2, 2)
+        gather(on_scalar, 3, 2)
+        gather(on_vector, 3, 1, (0,))
+        gather(on_scalar, 3, 1, (1,))
+        gather(on_scalar, 3, 0)
+
+        nc.vector.tensor_tensor(big[:, 0, :], second0[:], third0[:], ALU.max)
+        nc.vector.tensor_tensor(small[:, 0, :], second0[:], third0[:], ALU.min)
+        nc.vector.tensor_tensor(paired(big[:, 1, :]), by_target(1, 1), by_target(1, 2), ALU.max)
+        nc.vector.tensor_tensor(paired(small[:, 1, :]), by_target(1, 1), by_target(1, 2), ALU.min)
+        nc.scalar.copy(paired(first[:, 1, :]), by_target(1, 0))
+
         mean0 = tile("mean0", [P, 2, P, 2], BF16)
         nc.scalar.activation(mean0[:], total[0][:].rearrange("v h e p -> v h p e"), ACT.Copy, scale=1.0 / D)
         for half in range(2):
@@ -268,7 +249,7 @@ def tile_picked_pna_silu_p_kernel(
 
         zc = [tile("zc%d" % a, [P, V], U32) for a in range(D)]
         zs = [tile("zs%d" % a, [P, V], U8) for a in range(D)]
-        res = [ps.tile([P, P], F32, name="res%d" % half, tag="bank%d" % (3 + half)) for half in range(2)]
+        res = [bank("res%d" % half, [P, P], 3 + half) for half in range(2)]
 
         def second_product(a, half, start, stop):
             cols = slice(half * P, (half + 1) * P)

@@ -24,6 +24,7 @@ QUADRANTS = 4
 D = 3
 LIST_ROWS = 16
 HALF_M = P // 2
+SHARE_M = 3 * P // 4
 
 
 def tile_picked_pna_silu_p_kernel(
@@ -107,10 +108,10 @@ def tile_picked_pna_silu_p_kernel(
                 wc[z, u] = tile("wc%d_%d" % (z, u), [P, 2 * P], U32)
                 wsc[z, u] = tile("wsc%d_%d" % (z, u), [P, 2 * P], U8)
 
-        def round_w1(copy, raw, z, u, m0, m1):
+        def round_w1(copy, raw, z, u, m0, m1, first_m=0):
             copy(
                 wb[z, u][:, :, m0:m1, :].rearrange("p e m j -> p m j e"),
-                raw[:].rearrange("p j (m t) -> p m j t", t=PACK)[:, :, :, 2 * u : 2 * u + 2],
+                raw[:].rearrange("p j (m t) -> p m j t", t=PACK)[:, m0 - first_m : m1 - first_m, :, 2 * u : 2 * u + 2],
             )
 
         def quantise_w1(z, u, c0, c1):
@@ -125,13 +126,14 @@ def tile_picked_pna_silu_p_kernel(
         for u in range(2):
             quantise_w1(0, u, 0, 2 * P)
         nc.vector.tensor_copy(xw[1][:], xw_all[1][:].indirect(offs_sb[:]))
-        for u in range(2):
-            round_w1(nc.scalar.copy, w1_last[0], 1, u, 0, HALF_M)
-        round_w1(nc.vector.tensor_copy, w1_last[1], 1, 0, HALF_M, P)
+        round_w1(nc.scalar.copy, w1_last[0], 1, 0, 0, HALF_M)
+        round_w1(nc.vector.tensor_copy, w1_last[0], 1, 1, 0, HALF_M)
+        round_w1(nc.scalar.copy, w1_last[1], 1, 0, HALF_M, SHARE_M, HALF_M)
+        round_w1(nc.vector.tensor_copy, w1_last[1], 1, 0, SHARE_M, P, HALF_M)
         for m0 in (0, HALF_M):
             for e in range(2):
                 quantise_w1(1, 0, e * P + m0, e * P + m0 + HALF_M)
-        round_w1(nc.scalar.copy, w1_last[1], 1, 1, HALF_M, P)
+        round_w1(nc.scalar.copy, w1_last[1], 1, 1, HALF_M, P, HALF_M)
         quantise_w1(1, 1, 0, 2 * P)
 
         spans = [(0, 0, S // 2), (0, S // 2, S)] + [(t, 0, S) for t in range(1, PACK)]

@@ -222,8 +222,13 @@ def tile_picked_pna_silu_p_kernel(
 
         nc.vector.tensor_tensor(big[:, 0, :], second0[:], third0[:], ALU.max)
         nc.vector.tensor_tensor(small[:, 0, :], second0[:], third0[:], ALU.min)
-        nc.vector.tensor_tensor(paired(big[:, 1, :]), by_target(1, 1), by_target(1, 2), ALU.max)
-        nc.vector.tensor_tensor(paired(small[:, 1, :]), by_target(1, 1), by_target(1, 2), ALU.min)
+        for part, op in ((big, ALU.max), (small, ALU.min)):
+            nc.vector.tensor_tensor(
+                part[:, 1, :].rearrange("p (w i e) -> p w e i", i=4, e=2),
+                g[1][1][:].rearrange("p e (w i) -> p w e i", i=4),
+                g[1][2][:].rearrange("p e (w i) -> p w e i", i=4),
+                op,
+            )
         nc.scalar.copy(paired(first[:, 1, :]), by_target(1, 0))
 
         mean0 = tile("mean0", [P, 2, P, 2], BF16)

@@ -23,8 +23,7 @@ PASSES = K // K_PASS
 QUADRANTS = 4
 D = 3
 LIST_ROWS = 16
-HALF_M = P // 2
-SHARE_M = 3 * P // 4
+SHARE_M = P // 2
 
 
 def tile_picked_pna_silu_p_kernel(
@@ -72,7 +71,11 @@ def tile_picked_pna_silu_p_kernel(
             )
         w1_first = load_w1(0, 0, H)
         load_words(xw_all[1], x_words[1])
-        w1_last = [load_w1(1, 0, H // 2), load_w1(1, H // 2, H)]
+        w1_last = []
+        for i in range(2):
+            piece = tile("w1_last%d" % i, [P, 2, H], F32)
+            nc.sync.dma_start(piece[:], w1[K_PASS:, :].rearrange("(p j) c -> p j c", j=PACK)[:, 2 * i : 2 * i + 2, :])
+            w1_last.append(piece)
 
         pos_sb = []
         for d, pos in enumerate((pos1, pos2, pos3)):
@@ -126,14 +129,20 @@ def tile_picked_pna_silu_p_kernel(
         for u in range(2):
             quantise_w1(0, u, 0, 2 * P)
         nc.vector.tensor_copy(xw[1][:], xw_all[1][:].indirect(offs_sb[:]))
-        round_w1(nc.scalar.copy, w1_last[0], 1, 0, 0, HALF_M)
-        round_w1(nc.vector.tensor_copy, w1_last[0], 1, 1, 0, HALF_M)
-        round_w1(nc.scalar.copy, w1_last[1], 1, 0, HALF_M, SHARE_M, HALF_M)
-        round_w1(nc.vector.tensor_copy, w1_last[1], 1, 0, SHARE_M, P, HALF_M)
-        for m0 in (0, HALF_M):
-            for e in range(2):
-                quantise_w1(1, 0, e * P + m0, e * P + m0 + HALF_M)
-        round_w1(nc.scalar.copy, w1_last[1], 1, 1, HALF_M, P, HALF_M)
+
+        def round_last(copy, i, u, m0, m1):
+            copy(
+                wb[1, u][:, :, m0:m1, 2 * i : 2 * i + 2].rearrange("p e m j -> p m j e"),
+                w1_last[i][:].rearrange("p j (m t) -> p m j t", t=PACK)[:, m0:m1, :, 2 * u : 2 * u + 2],
+            )
+
+        round_last(nc.scalar.copy, 0, 0, 0, P)
+        round_last(nc.vector.tensor_copy, 0, 1, 0, P)
+        round_last(nc.scalar.copy, 1, 0, 0, SHARE_M)
+        round_last(nc.vector.tensor_copy, 1, 0, SHARE_M, P)
+        for e in range(2):
+            quantise_w1(1, 0, e * P, (e + 1) * P)
+        round_last(nc.scalar.copy, 1, 1, 0, P)
         quantise_w1(1, 1, 0, 2 * P)
 
         spans = [(0, 0, S // 2), (0, S // 2, S)] + [(t, 0, S) for t in range(1, PACK)]

@@ -23,7 +23,7 @@ PASSES = K // K_PASS
 QUADRANTS = 4
 D = 3
 LIST_ROWS = 16
-SHARE_M = P // 2
+SHARE_M = 40
 
 
 def tile_picked_pna_silu_p_kernel(
@@ -142,7 +142,8 @@ def tile_picked_pna_silu_p_kernel(
         round_last(nc.vector.tensor_copy, 1, 0, SHARE_M, P)
         for e in range(2):
             quantise_w1(1, 0, e * P, (e + 1) * P)
-        round_last(nc.scalar.copy, 1, 1, 0, P)
+        round_last(nc.scalar.copy, 1, 1, 0, P // 2)
+        round_last(nc.vector.tensor_copy, 1, 1, P // 2, P)
         quantise_w1(1, 1, 0, 2 * P)
 
         spans = [(0, 0, S // 2), (0, S // 2, S)] + [(t, 0, S) for t in range(1, PACK)]

@@ -36,7 +36,7 @@ def tile_picked_pna_silu_p_kernel(
         ps = ctx.enter_context(tc.psum_pool(name="ps", bufs=1))
 
         def tile(name, shape, dtype):
-            return sb.tile(shape, dtype, name=name, align_bytes=64)
+            return sb.tile(shape, dtype, name=name, align_bytes=256)
 
         def bank(name, shape, number):
             return ps.tile(shape, F32, name=name, tag="bank%d" % number)

@@ -41,6 +41,8 @@ def tile_picked_pna_silu_p_kernel(
         def bank(name, shape, number):
             return ps.tile(shape, F32, name=name, tag="bank%d" % number)
 
+        xs_all = tile("xs_all", [P, T], U8)
+        nc.gpsimd.memset(xs_all[:].bitcast(I32), 0)
         warm_in = tile("warm_in", [P, 8], F32)
         warm = tile("warm", [P, 8], F32)
         nc.gpsimd.memset(warm_in[:], 0.0)
@@ -48,8 +50,6 @@ def tile_picked_pna_silu_p_kernel(
 
         offs_sb = tile("offs_sb", [P, S // LIST_ROWS], U16)
 
-        xs_all = tile("xs_all", [P, T], U8)
-        nc.vector.memset(xs_all[:].bitcast(I32), 0)
         ws_all = tile("ws_all", [P, D * N], U8)
         nc.vector.memset(ws_all[:].bitcast(I32), 0)
 

@@ -138,8 +138,15 @@ def tile_picked_pna_silu_p_kernel(
 
         round_last(nc.scalar.copy, 0, 0, 0, P)
         round_last(nc.vector.tensor_copy, 0, 1, 0, P)
-        round_last(nc.scalar.copy, 1, 0, 0, SHARE_M)
-        round_last(nc.vector.tensor_copy, 1, 0, SHARE_M, P)
+        def round_last_tile(copy, e, m0, m1):
+            copy(
+                wb[1, 0][:, e, m0:m1, 2:],
+                w1_last[1][:].rearrange("p j (m t) -> p m j t", t=PACK)[:, m0:m1, :, e],
+            )
+
+        for e in range(2):
+            round_last_tile(nc.scalar.copy, e, 0, SHARE_M)
+            round_last_tile(nc.vector.tensor_copy, e, SHARE_M, P)
         for e in range(2):
             quantise_w1(1, 0, e * P, (e + 1) * P)
         round_last(nc.scalar.copy, 1, 1, 0, P // 2)

@@ -23,7 +23,7 @@ PASSES = K // K_PASS
 QUADRANTS = 4
 D = 3
 LIST_ROWS = 16
-SHARE_M = 40
+SHARE_M = 64
 
 
 def tile_picked_pna_silu_p_kernel(
@@ -248,14 +248,13 @@ def tile_picked_pna_silu_p_kernel(
             )
         nc.scalar.copy(paired(first[:, 1, :]), by_target(1, 0))
 
-        mean0 = tile("mean0", [P, 2, P, 2], BF16)
-        nc.scalar.activation(mean0[:], total[0][:].rearrange("v h e p -> v h p e"), ACT.Copy, scale=1.0 / D)
-        for half in range(2):
-            turn_back(0, half, mean0[:, half, :, :])
-        for half in range(2):
-            mean1 = tile("mean1_%d" % half, [P, P, 2], BF16)
-            nc.scalar.activation(mean1[:], total[1][:, half, :, :].rearrange("v e p -> v p e"), ACT.Copy, scale=1.0 / D)
-            turn_back(1, half, mean1[:])
+        for u in range(2):
+            for half in range(2):
+                mean = tile("mean%d_%d" % (u, half), [P, P, 2], BF16)
+                nc.scalar.activation(
+                    mean[:], total[u][:, half, :, :].rearrange("v e p -> v p e"), ACT.Copy, scale=1.0 / D
+                )
+                turn_back(u, half, mean[:])
 
         zb = [tile("zb%d" % a, [P, PACK * V], BF16) for a in range(D)]
         for a, part, op in ((1, big, ALU.max), (2, small, ALU.min)):

from contextlib import ExitStack

import concourse.mybir as mybir
from concourse.masks import make_identity

K, T, S, V, H, N = 1024, 1024, 512, 256, 512, 128
FLOPS = 2 * K * H * S + 3 * 2 * H * N * V

F32 = mybir.dt.float32
BF16 = mybir.dt.bfloat16
I32 = mybir.dt.int32
U32 = mybir.dt.uint32
U16 = mybir.dt.uint16
U8 = mybir.dt.uint8
FP8X4 = mybir.dt.float8_e4m3fn_x4
ACT = mybir.ActivationFunctionType
ALU = mybir.AluOpType

P = 128
PACK = 4
K_PASS = P * PACK
PASSES = K // K_PASS
QUADRANTS = 4
D = 3
LIST_ROWS = 16
SHARE_M = 64


def tile_picked_pna_silu_p_kernel(
    tc, x_words, x_scales, w1, w2_words, w2_scales, w3_words, w3_scales, w4_words, w4_scales,
    offs, pos1, pos2, pos3, out,
):
    nc = tc.nc
    with ExitStack() as ctx:
        sb = ctx.enter_context(tc.tile_pool(name="sb", bufs=1))
        ps = ctx.enter_context(tc.psum_pool(name="ps", bufs=1))

        def tile(name, shape, dtype):
            return sb.tile(shape, dtype, name=name, align_bytes=256)

        def bank(name, shape, number):
            return ps.tile(shape, F32, name=name, tag="bank%d" % number)

        xs_all = tile("xs_all", [P, T], U8)
        nc.gpsimd.memset(xs_all[:].bitcast(I32), 0)
        warm_in = tile("warm_in", [P, 8], F32)
        warm = tile("warm", [P, 8], F32)
        nc.gpsimd.memset(warm_in[:], 0.0)
        nc.scalar.activation(warm[:], warm_in[:], ACT.Silu)

        offs_sb = tile("offs_sb", [P, S // LIST_ROWS], U16)

        ws_all = tile("ws_all", [P, D * N], U8)
        nc.vector.memset(ws_all[:].bitcast(I32), 0)

        def load_words(dst, words):
            nc.sync.dma_start(dst[:].bitcast(I32), words.rearrange("p n t -> p (n t)").bitcast(I32))

        def load_w1(z, c0, c1):
            raw = tile("w1_raw%d_%d" % (z, c0), [P, PACK, c1 - c0], F32)
            nc.sync.dma_start(raw[:], w1[K_PASS * z : K_PASS * (z + 1), c0:c1].rearrange("(p j) c -> p j c", j=PACK))
            return raw

        xw_all = [tile("xw_all%d" % z, [P, T], U32) for z in range(PASSES)]
        load_words(xw_all[0], x_words[0])
        nc.sync.dma_start(offs_sb[:], offs)
        for q in range(QUADRANTS):
            nc.sync.dma_start(
                xs_all[32 * q : 32 * q + 4 * PASSES, :].bitcast(I32),
                x_scales[:, 4 * q : 4 * q + 4, :].bitcast(I32),
            )
        w1_first = load_w1(0, 0, H)
        load_words(xw_all[1], x_words[1])
        w1_last = []
        for i in range(2):
            piece = tile("w1_last%d" % i, [P, 2, H], F32)
            nc.sync.dma_start(piece[:], w1[K_PASS:, :].rearrange("(p j) c -> p j c", j=PACK)[:, 2 * i : 2 * i + 2, :])
            w1_last.append(piece)

        pos_sb = []
        for d, pos in enumerate((pos1, pos2, pos3)):
            lst = tile("pos_sb%d" % d, [P, V // LIST_ROWS], U16)
            nc.sync.dma_start(lst[:], pos)
            pos_sb.append(lst)

        ww = []
        for a, (words, scales) in enumerate(((w2_words, w2_scales), (w3_words, w3_scales), (w4_words, w4_scales))):
            wt = tile("ww%d" % a, [P, N], U32)
            load_words(wt, words[0])
            ww.append(wt)
            for q in range(QUADRANTS):
                nc.sync.dma_start(
                    ws_all[32 * q : 32 * q + 4, a * N : (a + 1) * N].bitcast(I32),
                    scales[0, 4 * q : 4 * q + 4, :].bitcast(I32),
                )

        ident = tile("ident", [P, P], F32)
        make_identity(nc, ident[:])

        xw = [tile("xw%d" % z, [P, S], U32) for z in range(PASSES)]
        xs = tile("xs", [P, S], U8)
        nc.vector.tensor_copy(xw[0][:], xw_all[0][:].indirect(offs_sb[:]))
        nc.vector.tensor_copy(xs[:], xs_all[:].indirect(offs_sb[:]))

        wb = {}
        wc = {}
        wsc = {}
        for z in range(PASSES):
            for u in range(2):
                wb[z, u] = tile("wb%d_%d" % (z, u), [P, 2, P, PACK], BF16)
                wc[z, u] = tile("wc%d_%d" % (z, u), [P, 2 * P], U32)
                wsc[z, u] = tile("wsc%d_%d" % (z, u), [P, 2 * P], U8)

        def round_w1(copy, raw, z, u, m0, m1, first_m=0):
            copy(
                wb[z, u][:, :, m0:m1, :].rearrange("p e m j -> p m j e"),
                raw[:].rearrange("p j (m t) -> p m j t", t=PACK)[:, m0 - first_m : m1 - first_m, :, 2 * u : 2 * u + 2],
            )

        def quantise_w1(z, u, c0, c1):
            nc.vector.quantize_mx(
                out=wc[z, u][:, c0:c1].bitcast(FP8X4),
                scales=wsc[z, u][:, c0:c1],
                in_=wb[z, u][:].rearrange("p e m j -> p (e m j)")[:, c0 * PACK : c1 * PACK],
            )

        round_w1(nc.vector.tensor_copy, w1_first, 0, 0, 0, P)
        round_w1(nc.scalar.copy, w1_first, 0, 1, 0, P)
        for u in range(2):
            quantise_w1(0, u, 0, 2 * P)
        nc.vector.tensor_copy(xw[1][:], xw_all[1][:].indirect(offs_sb[:]))

        def round_last(copy, i, u, m0, m1):
            copy(
                wb[1, u][:, :, m0:m1, 2 * i : 2 * i + 2].rearrange("p e m j -> p m j e"),
                w1_last[i][:].rearrange("p j (m t) -> p m j t", t=PACK)[:, m0:m1, :, 2 * u : 2 * u + 2],
            )

        round_last(nc.scalar.copy, 0, 0, 0, P)
        round_last(nc.vector.tensor_copy, 0, 1, 0, P)
        def round_last_tile(copy, e, m0, m1):
            copy(
                wb[1, 0][:, e, m0:m1, 2:],
                w1_last[1][:].rearrange("p j (m t) -> p m j t", t=PACK)[:, m0:m1, :, e],
            )

        for e in range(2):
            round_last_tile(nc.scalar.copy, e, 0, SHARE_M)
            round_last_tile(nc.vector.tensor_copy, e, SHARE_M, P)
        for e in range(2):
            quantise_w1(1, 0, e * P, (e + 1) * P)
        round_last(nc.scalar.copy, 1, 1, 0, P // 2)
        round_last(nc.vector.tensor_copy, 1, 1, P // 2, P)
        quantise_w1(1, 1, 0, 2 * P)

        spans = [(0, 0, S // 2), (0, S // 2, S)] + [(t, 0, S) for t in range(1, PACK)]
        h = [tile("h%d" % t, [P, S], F32) for t in range(PACK)]
        accs = []
        for i, (t, c0, c1) in enumerate(spans):
            u, e = divmod(t, 2)
            acc = bank("acc%d" % i, [P, c1 - c0], i)
            for z in range(PASSES):
                nc.tensor.matmul_mx(
                    out=acc[:],
                    lhsT=wc[z, u][:, e * P : (e + 1) * P].bitcast(FP8X4),
                    lhsT_scale=wsc[z, u][:, e * P : (e + 1) * P],
                    rhs=xw[z][:, c0:c1].bitcast(FP8X4),
                    rhs_scale=xs[4 * z :, c0:c1],
                    start=(z == 0),
                    stop=(z == PASSES - 1),
                )
            accs.append(acc)

        def silu(t):
            for acc, (tile_of_span, c0, c1) in zip(accs, spans):
                if tile_of_span == t:
                    nc.scalar.activation(h[t][:, c0:c1], acc[:], ACT.Silu)

        g = [[tile("g%d_%d" % (u, d), [P, 2, V], F32) for d in range(D)] for u in range(2)]

        total = [bank("total%d" % u, [P, 2, 2, P], len(spans) + u) for u in range(2)]
        added = [0, 0]

        def add_turned(t, d, halves):
            u, e = divmod(t, 2)
            for half in halves:
                nc.tensor.matmul(
                    total[u][:, half, e, :], lhsT=g[u][d][:, e, half * P : (half + 1) * P], rhs=ident[:],
                    is_transpose=True, start=(added[u] == 0), stop=(added[u] == 4 * D - 1),
                )
                added[u] = added[u] + 1

        def scalar_copy(dst, src):
            nc.scalar.activation(dst, src, ACT.Copy)

        def gather(copy, t, d, halves=(0, 1)):
            v0, v1 = halves[0] * P, (halves[-1] + 1) * P
            offsets = pos_sb[d][:, v0 // LIST_ROWS : v1 // LIST_ROWS]
            copy(g[t // 2][d][:, t % 2, v0:v1], h[t][:].indirect(offsets))
            add_turned(t, d, halves)

        big = tile("big", [P, 2, 2 * V], BF16)
        small = tile("small", [P, 2, 2 * V], BF16)
        first = tile("first", [P, 2, 2 * V], BF16)
        second0 = tile("second0", [P, 2 * V], BF16)
        third0 = tile("third0", [P, 2 * V], BF16)
        back = [bank("back%d" % half, [P, 2, P], number) for half, number in enumerate((2, 7))]

        def paired(ap):
            return ap.rearrange("p (v e) -> p v e", e=2)

        def by_target(u, d):
            return g[u][d][:].rearrange("p e v -> p v e")

        def turn_back(u, half, mean_half):
            nc.tensor.transpose(back[half][:, u, :], mean_half.rearrange("v p e -> v (p e)").bitcast(F32), ident[:])

        on_vector, on_scalar = nc.vector.tensor_copy, scalar_copy
        silu(0)
        gather(on_vector, 0, 1)
        silu(1)
        gather(on_scalar, 0, 0)
        gather(on_vector, 1, 1)
        nc.gpsimd.tensor_copy(paired(second0[:]), by_target(0, 1))
        silu(2)
        gather(on_scalar, 0, 2)
        gather(on_vector, 1, 0)
        nc.gpsimd.tensor_copy(paired(first[:, 0, :]), by_target(0, 0))
        gather(on_vector, 1, 2)
        nc.gpsimd.tensor_copy(paired(third0[:]), by_target(0, 2))
        silu(3)
        gather(on_vector, 2, 1)
        gather(on_scalar, 2, 0)
        gather(on_vector, 2, 2)
        gather(on_scalar, 3, 2)
        gather(on_vector, 3, 1, (0,))
        gather(on_scalar, 3, 1, (1,))
        gather(on_scalar, 3, 0)

        nc.vector.tensor_tensor(big[:, 0, :], second0[:], third0[:], ALU.max)
        nc.vector.tensor_tensor(small[:, 0, :], second0[:], third0[:], ALU.min)
        for part, op in ((big, ALU.max), (small, ALU.min)):
            nc.vector.tensor_tensor(
                part[:, 1, :].rearrange("p (w i e) -> p w e i", i=4, e=2),
                g[1][1][:].rearrange("p e (w i) -> p w e i", i=4),
                g[1][2][:].rearrange("p e (w i) -> p w e i", i=4),
                op,
            )
        nc.scalar.copy(paired(first[:, 1, :]), by_target(1, 0))

        for u in range(2):
            for half in range(2):
                mean = tile("mean%d_%d" % (u, half), [P, P, 2], BF16)
                nc.scalar.activation(
                    mean[:], total[u][:, half, :, :].rearrange("v e p -> v p e"), ACT.Copy, scale=1.0 / D
                )
                turn_back(u, half, mean[:])

        zb = [tile("zb%d" % a, [P, PACK * V], BF16) for a in range(D)]
        for a, part, op in ((1, big, ALU.max), (2, small, ALU.min)):
            nc.vector.tensor_tensor(
                zb[a][:].rearrange("p (v u e) -> p v u e", u=2, e=2),
                part[:].rearrange("p u (v e) -> p v u e", e=2),
                first[:].rearrange("p u (v e) -> p v u e", e=2),
                op,
            )
        for half in range(2):
            nc.scalar.copy(
                zb[0][:, half * P * PACK : (half + 1) * P * PACK].bitcast(F32).rearrange("p (v u) -> p v u", u=2),
                back[half][:].rearrange("p u v -> p v u"),
            )

        zc = [tile("zc%d" % a, [P, V], U32) for a in range(D)]
        zs = [tile("zs%d" % a, [P, V], U8) for a in range(D)]
        res = [bank("res%d" % half, [P, P], 3 + half) for half in range(2)]

        def second_product(a, half, start, stop):
            cols = slice(half * P, (half + 1) * P)
            nc.tensor.matmul_mx(
                out=res[half][:], lhsT=ww[a][:].bitcast(FP8X4), lhsT_scale=ws_all[:, a * N : (a + 1) * N],
                rhs=zc[a][:, cols].bitcast(FP8X4), rhs_scale=zs[a][:, cols], start=start, stop=stop,
            )

        for a in (1, 2):
            nc.vector.quantize_mx(out=zc[a][:].bitcast(FP8X4), scales=zs[a][:], in_=zb[a][:])
            for half in range(2):
                second_product(a, half, a == 1, False)
        for half, copy in ((0, nc.scalar.copy), (1, nc.vector.tensor_copy)):
            cols = slice(half * P, (half + 1) * P)
            nc.vector.quantize_mx(
                out=zc[0][:, cols].bitcast(FP8X4), scales=zs[0][:, cols],
                in_=zb[0][:, half * P * PACK : (half + 1) * P * PACK],
            )
            second_product(0, half, False, True)
            res_sb = tile("res_sb%d" % half, [P, P], F32)
            copy(res_sb[:], res[half][:])
            nc.sync.dma_start(out[:, cols], res_sb[:])
